import numpy as np
import ml_dtypes


def mxq(x, axis, fmt="e4m3"):
    dtype, down = {"e4m3": (ml_dtypes.float8_e4m3fn, 7), "e5m2": (ml_dtypes.float8_e5m2, 14)}[fmt]
    v = np.moveaxis(np.asarray(x, np.float32).astype(ml_dtypes.bfloat16).astype(np.float64), axis, -1)
    blocks = v.reshape(v.shape[:-1] + (-1, 32))
    amax = np.abs(blocks).max(-1, keepdims=True)
    byte = np.maximum(np.where(amax > 0, np.frexp(amax)[1] - 1 + 127, 0) - down, 1)
    scale = np.exp2(byte - 127.0)
    codes = (blocks / scale).astype(np.float32).astype(dtype).astype(np.float64)
    return np.moveaxis((codes * scale).reshape(v.shape), -1, axis)


WIDE = False


def mx_kscale(k):
    if not WIDE:
        return np.ones(k)
    levels = np.array([10, -10, 5, -5, 0])
    if k % 512:
        return np.exp2(np.random.permutation(np.resize(levels, k // 32))).repeat(32)
    a = np.empty((k // 512, 16))
    for p in range(k // 512):
        a[p, :8] = np.random.permutation(np.resize(levels, 8))
        for g in range(8):
            far = levels[np.abs(levels - a[p, g]) >= 10]
            a[p, g + 8] = far[np.random.randint(len(far))]
    return np.exp2(a.ravel()).repeat(32)


def f64(x):
    return np.asarray(x).astype(np.float64)


def striped(idx):
    return np.tile(idx.reshape(-1, 16).T, (8, 1)).astype(np.uint16)


def unstriped(offs):
    return offs[:16].T.reshape(-1).astype(np.int64)


E2M1 = np.array([0.0, 0.5, 1.0, 1.5, 2.0, 3.0, 4.0, 6.0, -0.0, -0.5, -1.0, -1.5, -2.0, -3.0, -4.0, -6.0])


def pack_weight(w, fmt):
    k, n = w.shape
    w = f64(np.asarray(w, np.float32).astype(ml_dtypes.bfloat16)).reshape(k // 32, 32, n)
    amax = np.abs(w).max(1)
    if fmt == "e4m3":
        byte = np.frexp(amax)[1] - 1 + 127 - 7
    else:
        mant, ex = np.frexp(amax / 6.0)
        byte = np.where(mant > 0.5, ex, ex - 1) + 127
    byte = np.clip(np.where(amax > 0, byte, 1), 1, 254)
    scaled = (w * np.exp2(127.0 - byte)[:, None, :]).reshape(k, n).astype(np.float32)
    by_word = np.ascontiguousarray(scaled.reshape(k // 512, 128, 4, n).transpose(0, 1, 3, 2))
    if fmt == "e4m3":
        words = by_word.astype(ml_dtypes.float8_e4m3fn).view(np.uint8)
    else:
        c = by_word.astype(ml_dtypes.float4_e2m1fn).view(np.uint8) & 0xF
        words = (c[..., 0::2] | (c[..., 1::2] << 4)).reshape(k // 512, 128, 2 * n)
    return np.ascontiguousarray(words), np.ascontiguousarray(byte.astype(np.uint8).reshape(k // 512, 16, n))


def unpack_weight(words, scales, fmt):
    g, _, n = scales.shape
    words = np.ascontiguousarray(words).reshape(g, 128, n, -1)
    if fmt == "e4m3":
        vals = words.view(ml_dtypes.float8_e4m3fn).astype(np.float64)
    else:
        nib = np.empty((g, 128, n, 4), np.uint8)
        nib[..., 0::2] = words & 0xF
        nib[..., 1::2] = words >> 4
        vals = E2M1[nib]
    vals = vals * np.repeat(np.exp2(scales.astype(np.float64) - 127.0), 8, axis=1)[..., None]
    return vals.transpose(0, 1, 3, 2).reshape(g * 512, n)


def gelu(v):
    return 0.5 * v * (1.0 + np.tanh(np.sqrt(2.0 / np.pi) * (v + 0.044715 * v**3)))


K, H, T, S, T2, P = 1024, 512, 4096, 1024, 2048, 1024

def setup_inputs():
    n = np.random.standard_normal
    s = mx_kscale(K)[:, None]
    u = mx_kscale(H)[:, None]
    d = {}
    d["tab_words"], d["tab_scales"] = pack_weight(n((K, T)) * s, "e4m3")
    d["offs"] = striped(np.random.permutation(T)[:S])
    d["w1_words"], d["w1_scales"] = pack_weight(1.2 * n((K, H)) / K**0.5 / s * u.T, "e2m1")
    d["w2"] = (1.8 * n((K, H)) / K**0.5 / s).astype(np.float32)
    d["w3"] = (0.8 * n((K, H)) / K**0.5 / s * u.T).astype(np.float32)
    d["wgs"] = np.exp(0.3 * n((128, S))).astype(np.float32)
    d["page0"] = (1.2 * n((H, T2)) * u).astype(np.float32)
    d["offs2"] = striped(np.random.permutation(T2)[:S])
    d["offs3"] = striped(np.random.permutation(T2)[:P])
    d["offs4"] = striped(np.random.permutation(T2)[:P])
    d["gx"] = np.exp(0.3 * n(H)).astype(np.float32)
    d["site"] = (0.8 * n((H, P)) * u).astype(np.float32)
    d["w4_words"], d["w4_scales"] = pack_weight(0.9 * n((H, H)) / H**0.5 / u, "e4m3")
    d["gy"] = (np.exp(0.3 * n(H)) / u[:, 0]).astype(np.float32)
    return d

def reference(tab_words, tab_scales, offs, w1_words, w1_scales, w2, w3, wgs, page0, offs2, offs3, offs4, gx, site, w4_words, w4_scales, gy):
    v = unpack_weight(tab_words, tab_scales, "e4m3")[:, unstriped(offs)]
    a = unpack_weight(w1_words, w1_scales, "e2m1").T @ v
    b = mxq(f64(w2), 0, "e4m3").T @ v
    e = mxq(f64(w3), 0, "e4m3").T @ v
    h = np.abs(a) * np.tanh(b) + e
    page = f64(page0).copy()
    page[:, unstriped(offs2)] = np.tile(f64(wgs), (H // 128, 1)) * h
    x = f64(gx)[:, None] * page[:, unstriped(offs3)] + f64(site)
    y = unpack_weight(w4_words, w4_scales, "e4m3").T @ mxq(x, 0, "e4m3")
    peer = f64(gy)[:, None] * page[:, unstriped(offs4)]
    return np.tanh(y) * peer + y

@@ -1,0 +1,280 @@
+from contextlib import ExitStack
+
+import concourse.mybir as mybir
+from concourse.masks import make_identity
+
+K, H, T, S, T2, PJ = 1024, 512, 4096, 1024, 2048, 1024
+FLOPS = 2 * (3 * K * H * S + H * H * PJ)
+
+F32 = mybir.dt.float32
+BF16 = mybir.dt.bfloat16
+I32 = mybir.dt.int32
+U32 = mybir.dt.uint32
+U16 = mybir.dt.uint16
+U8 = mybir.dt.uint8
+FP8X4 = mybir.dt.float8_e4m3fn_x4
+FP4X4 = mybir.dt.float4_e2m1fn_x4
+ACT = mybir.ActivationFunctionType
+ALU = mybir.AluOpType
+
+P = 128
+PASSES = K // 512
+TILES = H // P
+HALF = 512
+CH = 256
+CHUNKS = PJ // CH
+
+
+def tile_list_cryogen_board_scores_kernel(
+    tc, tab_words, tab_scales, offs, w1_words, w1_scales, w2, w3, wgs, page0,
+    offs2, offs3, offs4, gx, site, w4_words, w4_scales, gy, out,
+):
+    nc = tc.nc
+    with ExitStack() as ctx:
+        held = ctx.enter_context(tc.tile_pool(name="held", bufs=1))
+        work = ctx.enter_context(tc.tile_pool(name="work", bufs=2))
+        psum = ctx.enter_context(tc.psum_pool(name="psum", bufs=1))
+
+        def entries(lst, first, count):
+            return lst[:, first // 16 : (first + count) // 16]
+
+        list1 = held.tile([P, S // 16], U16, name="list1")
+        nc.sync.dma_start(list1[:], offs)
+        scale_window = held.tile([P, T], U8, name="scale_window")
+        nc.sync.dma_start(
+            out=scale_window[0:32, :].bitcast(I32),
+            in_=tab_scales.rearrange("a q t -> (a q) t").bitcast(I32),
+        )
+        nc.vector.memset(scale_window[32:64, :].bitcast(I32), 0)
+        nc.vector.memset(scale_window[64:128, :].bitcast(I32), 0)
+
+        warm_in = held.tile([P, 1], F32, name="warm_in")
+        warm_out = held.tile([P, 1], F32, name="warm_out")
+        nc.vector.memset(warm_in[:], 0.0)
+        nc.scalar.activation(warm_out[:], warm_in[:], ACT.Tanh)
+
+        w1_planes = held.tile([P, PASSES, H], U8, name="w1_planes", align_bytes=64)
+        nc.gpsimd.memset(w1_planes[:].rearrange("p a c -> p (a c)").bitcast(I32), 0)
+        tab_planes = [held.tile([P, S], U8, name=f"tab_plane{a}", align_bytes=64) for a in range(PASSES)]
+        for a in range(PASSES):
+            nc.gpsimd.memset(tab_planes[a][:].bitcast(I32), 0)
+        w4_plane = held.tile([P, H], U8, name="w4_plane", align_bytes=64)
+        nc.gpsimd.memset(w4_plane[:].bitcast(I32), 0)
+
+        word_windows = [held.tile([P, T], I32, name=f"word_window{a}", tag=f"window{a}") for a in range(PASSES)]
+
+        def load_words(a):
+            nc.sync.dma_start(out=word_windows[a][:], in_=tab_words[a].rearrange("p t i -> p (t i)").bitcast(I32))
+
+        raw = {}
+
+        def load_weights(b):
+            for a in range(PASSES):
+                for w, weight in enumerate((w2, w3)):
+                    t = work.tile([P, 4, P], F32, name=f"raw{b}{a}{w}", tag="raw", bufs=8)
+                    rows = weight[512 * a : 512 * (a + 1), P * b : P * (b + 1)]
+                    nc.sync.dma_start(out=t[:], in_=rows.rearrange("(p i) c -> p i c", i=4))
+                    raw[b, a, w] = t
+
+        load_words(0)
+        w1_codes = held.tile([P, PASSES, 2 * H], U8, name="w1_codes", align_bytes=64)
+        nc.sync.dma_start(out=w1_codes[:].bitcast(I32), in_=w1_words.rearrange("a p n -> p a n").bitcast(I32))
+        load_weights(0)
+        load_words(1)
+        for q in range(4):
+            nc.scalar.dma_start(
+                out=w1_planes[32 * q : 32 * q + 4, :, :].bitcast(I32),
+                in_=w1_scales[:, 4 * q : 4 * q + 4, :].rearrange("a r c -> r a c").bitcast(I32),
+            )
+        list2 = held.tile([P, S // 16], U16, name="list2")
+        nc.sync.dma_start(list2[:], offs2)
+        wgs_t = held.tile([P, S], F32, name="wgs_t", tag="wgs_then_picks")
+        nc.sync.dma_start(out=wgs_t[:], in_=wgs)
+        pages = [held.tile([P, T2], F32, name=f"page{b}") for b in range(TILES)]
+
+        def load_page(b):
+            nc.sync.dma_start(out=pages[b][:], in_=page0[P * b : P * (b + 1), :])
+
+        load_page(0)
+        load_weights(1)
+
+        picked_scales = held.tile([P, S], U8, name="picked_scales")
+        nc.vector.tensor_copy(picked_scales[:], scale_window[:].indirect(list1[:]))
+        for a in range(PASSES):
+            for q in range(4):
+                nc.gpsimd.dma_start(
+                    out=tab_planes[a][32 * q : 32 * q + 4, :].bitcast(I32),
+                    in_=picked_scales[16 * a + 4 * q : 16 * a + 4 * q + 4, :].bitcast(I32),
+                )
+        picked = {}
+        for a in range(PASSES):
+            for hf in range(2):
+                t = held.tile([P, HALF], U32, name=f"picked{a}{hf}", align_bytes=64)
+                nc.vector.tensor_copy(t[:], word_windows[a][:].bitcast(U32).indirect(entries(list1, HALF * hf, HALF)))
+                picked[a, hf] = t
+
+        ident = held.tile([P, P], F32, name="ident")
+        make_identity(nc, ident[:])
+
+        codes = {}
+        planes = {}
+
+        def quantise_weights(b):
+            for a in range(PASSES):
+                rounded = held.tile([P, 2, P, 4], BF16, name=f"rounded{b}{a}", tag=f"rounded{b}{a}", align_bytes=64)
+                for w in range(2):
+                    nc.scalar.copy(
+                        rounded[:, w, :, :].rearrange("p (g c) i -> p g i c", c=4),
+                        raw[b, a, w][:].rearrange("p i (g c) -> p g i c", c=4),
+                    )
+                codes[b, a] = held.tile([P, 2 * P], U32, name=f"codes{b}{a}", align_bytes=64)
+                planes[b, a] = held.tile([P, 2 * P], U8, name=f"planes{b}{a}", align_bytes=64)
+                nc.vector.quantize_mx(
+                    out=codes[b, a][:].bitcast(FP8X4),
+                    scales=planes[b, a][:],
+                    in_=rounded[:].rearrange("p w c i -> p (w c i)"),
+                )
+
+        def products(b, hf):
+            banks = [psum.tile([P, HALF], F32, name=f"acc{b}{hf}{n}", tag="acc", bufs=6) for n in range(3)]
+            cols = slice(HALF * hf, HALF * (hf + 1))
+            for a in range(PASSES):
+                stationary = [
+                    (codes[b, a][:, 0:P].bitcast(FP8X4), planes[b, a][:, 0:P]),
+                    (w1_codes[:, a, 2 * P * b : 2 * P * (b + 1)].bitcast(FP4X4), w1_planes[:, a, P * b : P * (b + 1)]),
+                    (codes[b, a][:, P : 2 * P].bitcast(FP8X4), planes[b, a][:, P : 2 * P]),
+                ]
+                for bank, (lhs, lhs_scale) in zip(banks, stationary):
+                    nc.tensor.matmul_mx(
+                        out=bank[:], lhsT=lhs, lhsT_scale=lhs_scale,
+                        rhs=picked[a, hf][:].bitcast(FP8X4), rhs_scale=tab_planes[a][:, cols],
+                        start=(a == 0), stop=(a == PASSES - 1),
+                    )
+            tanh_b = work.tile([P, HALF], F32, name=f"tanh_b{b}{hf}", tag="tanh_b")
+            nc.scalar.activation(tanh_b[:], banks[0][:], ACT.Tanh)
+            abs_a = work.tile([P, HALF], F32, name=f"abs_a{b}{hf}", tag="abs_a")
+            nc.scalar.activation(abs_a[:], banks[1][:], ACT.Abs)
+            return abs_a, tanh_b, banks[2]
+
+        quantise_weights(0)
+        for b in range(TILES):
+            parts = [products(b, hf) for hf in range(2)]
+            for abs_a, tanh_b, e_bank in parts:
+                nc.vector.tensor_tensor(abs_a[:], abs_a[:], tanh_b[:], ALU.mult)
+            if b == 0:
+                load_weights(2)
+                load_page(1)
+            if b == 1:
+                load_weights(3)
+                load_page(2)
+                load_page(3)
+            hs = []
+            for hf in range(2):
+                if hf == 1 and b + 1 < TILES:
+                    quantise_weights(b + 1)
+                    h = held.tile([P, HALF], F32, name=f"h{b}{hf}", tag=f"rounded{b + 1}1", align_bytes=64)
+                else:
+                    h = work.tile([P, HALF], F32, name=f"h{b}{hf}", tag="h")
+                nc.vector.tensor_tensor(h[:], parts[hf][0][:], parts[hf][2][:], ALU.add)
+                hs.append(h)
+            for hf in range(2):
+                cols = slice(HALF * hf, HALF * (hf + 1))
+                nc.vector.tensor_tensor(
+                    pages[b][:].indirect(entries(list2, HALF * hf, HALF)), hs[hf][:], wgs_t[:, cols], ALU.mult
+                )
+
+        site_t = held.tile([P, TILES, PJ], F32, name="site_t", tag="window0")
+        for b in range(TILES):
+            nc.sync.dma_start(out=site_t[:, b, :], in_=site[P * b : P * (b + 1), :])
+        list3 = held.tile([P, PJ // 16], U16, name="list3")
+        nc.sync.dma_start(list3[:], offs3)
+        list4 = held.tile([P, PJ // 16], U16, name="list4")
+        nc.sync.dma_start(list4[:], offs4)
+        w4_codes = held.tile([P, H], I32, name="w4_codes", align_bytes=64)
+        nc.sync.dma_start(out=w4_codes[:], in_=w4_words[0].rearrange("p c i -> p (c i)").bitcast(I32))
+        for q in range(4):
+            nc.sync.dma_start(
+                out=w4_plane[32 * q : 32 * q + 4, :].bitcast(I32),
+                in_=w4_scales[0, 4 * q : 4 * q + 4, :].bitcast(I32),
+            )
+        gx_t = held.tile([P, TILES], F32, name="gx_t")
+        gy_t = held.tile([P, TILES], F32, name="gy_t")
+        with nc.allow_non_contiguous_dma(reason="one gain a partition"):
+            nc.sync.dma_start(out=gx_t[:], in_=gx.rearrange("(b p) -> p b", p=P))
+            nc.sync.dma_start(out=gy_t[:], in_=gy.rearrange("(b p) -> p b", p=P))
+
+        first_picks = held.tile([P, (CHUNKS - 1) * TILES, CH], F32, name="first_picks", tag="wgs_then_picks")
+
+        def gather_x(c, picks):
+            for b in range(TILES):
+                nc.vector.tensor_copy(picks[b], pages[b][:].indirect(entries(list3, CH * c, CH)))
+
+        def make_x(c, picks):
+            for b in range(TILES):
+                nc.scalar.activation(picks[b], picks[b], ACT.Copy, scale=gx_t[:, b : b + 1])
+            turned = work.tile([P, CH // P, 2, P, 2], BF16, name=f"turned{c}", tag="turned")
+            for jb in range(CH // P):
+                bank = psum.tile([P, H], F32, name=f"turn{c}{jb}", tag="turn", bufs=2)
+                j0 = CH * c + P * jb
+                for b in range(TILES):
+                    nc.tensor.matmul(
+                        bank[:, P * b : P * (b + 1)], lhsT=site_t[:, b, j0 : j0 + P], rhs=ident[:],
+                        is_transpose=True, start=(b == 0), stop=False,
+                    )
+                for b in range(TILES):
+                    nc.tensor.matmul(
+                        bank[:, P * b : P * (b + 1)], lhsT=picks[b][:, P * jb : P * (jb + 1)], rhs=ident[:],
+                        is_transpose=True, start=False, stop=(b == TILES - 1),
+                    )
+                nc.scalar.copy(turned[:, jb, :, :, :], bank[:].rearrange("j (p u e) -> j u p e", u=2, e=2))
+            words = turned[:].rearrange("j g u p e -> j (g u p e)").bitcast(F32)
+            back = psum.tile([P, CH // P, 2, P], F32, name=f"back{c}", tag="acc", bufs=6)
+            for jb in range(CH // P):
+                for u in range(2):
+                    w0 = (2 * jb + u) * P
+                    nc.tensor.transpose(back[:, jb, u, :], words[:, w0 : w0 + P], ident[:])
+            x_in = held.tile([P, 4 * CH], BF16, name=f"x_in{c}", tag=f"x_in{c}", align_bytes=64)
+            nc.scalar.copy(
+                x_in[:].bitcast(F32).rearrange("p (g j u) -> p g j u", j=P, u=2),
+                back[:].rearrange("p g u j -> p g j u"),
+            )
+            x_codes = held.tile([P, CH], U32, name=f"x_codes{c}", align_bytes=64)
+            x_plane = held.tile([P, CH], U8, name=f"x_plane{c}", align_bytes=64)
+            nc.vector.quantize_mx(out=x_codes[:].bitcast(FP8X4), scales=x_plane[:], in_=x_in[:])
+            return x_codes, x_plane
+
+        def finish(c, x_codes, x_plane):
+            for pair in range(TILES // 2):
+                y = psum.tile([P, 2, CH], F32, name=f"y{c}{pair}", tag="acc", bufs=6)
+                for i in range(2):
+                    n0 = P * (2 * pair + i)
+                    nc.tensor.matmul_mx(
+                        out=y[:, i, :], lhsT=w4_codes[:, n0 : n0 + P].bitcast(FP8X4), lhsT_scale=w4_plane[:, n0 : n0 + P],
+                        rhs=x_codes[:].bitcast(FP8X4), rhs_scale=x_plane[:], start=True, stop=True,
+                    )
+                tanh_y = work.tile([P, 2, CH], F32, name=f"tanh_y{c}{pair}", tag="tanh_y", bufs=4)
+                nc.scalar.activation(tanh_y[:], y[:], ACT.Tanh)
+                peer = work.tile([P, 2, CH], F32, name=f"peer{c}{pair}", tag="peer")
+                for i in range(2):
+                    nc.vector.tensor_tensor(
+                        peer[:, i, :], pages[2 * pair + i][:].indirect(entries(list4, CH * c, CH)), tanh_y[:, i, :], ALU.mult
+                    )
+                for i in range(2):
+                    n = 2 * pair + i
+                    res = work.tile([P, CH], F32, name=f"res{c}{n}", tag="res", bufs=8)
+                    nc.vector.scalar_tensor_tensor(
+                        res[:], peer[:, i, :], gy_t[:, n : n + 1], y[:, i, :], ALU.mult, ALU.add
+                    )
+                    nc.sync.dma_start(out=out[P * n : P * (n + 1), CH * c : CH * (c + 1)], in_=res[:])
+
+        picks = {c: [first_picks[:, TILES * c + b, :] for b in range(TILES)] for c in range(CHUNKS - 1)}
+        for c in range(CHUNKS - 1):
+            gather_x(c, picks[c])
+        quantised = {0: make_x(0, picks[0])}
+        last_picks = held.tile([P, TILES, CH], F32, name="last_picks", tag="x_in0", align_bytes=64)
+        picks[CHUNKS - 1] = [last_picks[:, b, :] for b in range(TILES)]
+        gather_x(CHUNKS - 1, picks[CHUNKS - 1])
+        for c in range(CHUNKS):
+            if c + 1 < CHUNKS:
+                quantised[c + 1] = make_x(c + 1, picks[c + 1])
+            finish(c, *quantised[c])

@@ -69,27 +69,27 @@ def tile_list_cryogen_board_scores_kernel(
         raw = {}
 
         def load_weights(b):
-            for a in range(PASSES):
-                for w, weight in enumerate((w2, w3)):
+            for w, weight in enumerate((w2, w3)):
+                for a in range(PASSES):
                     t = work.tile([P, 4, P], F32, name=f"raw{b}{a}{w}", tag="raw", bufs=8)
                     rows = weight[512 * a : 512 * (a + 1), P * b : P * (b + 1)]
                     nc.sync.dma_start(out=t[:], in_=rows.rearrange("(p i) c -> p i c", i=4))
                     raw[b, a, w] = t
 
         load_words(0)
+        load_words(1)
         w1_codes = held.tile([P, PASSES, 2 * H], U8, name="w1_codes", align_bytes=64)
         nc.sync.dma_start(out=w1_codes[:].bitcast(I32), in_=w1_words.rearrange("a p n -> p a n").bitcast(I32))
         load_weights(0)
-        load_words(1)
         for q in range(4):
-            nc.scalar.dma_start(
+            nc.gpsimd.dma_start(
                 out=w1_planes[32 * q : 32 * q + 4, :, :].bitcast(I32),
                 in_=w1_scales[:, 4 * q : 4 * q + 4, :].rearrange("a r c -> r a c").bitcast(I32),
             )
         list2 = held.tile([P, S // 16], U16, name="list2")
         nc.sync.dma_start(list2[:], offs2)
         wgs_t = held.tile([P, S], F32, name="wgs_t", tag="wgs_then_picks")
-        nc.sync.dma_start(out=wgs_t[:], in_=wgs)
+        nc.sync.dma_start(out=wgs_t[:, 0:HALF], in_=wgs[:, 0:HALF])
         pages = [held.tile([P, T2], F32, name=f"page{b}") for b in range(TILES)]
 
         def load_page(b):
@@ -97,6 +97,7 @@ def tile_list_cryogen_board_scores_kernel(
 
         load_page(0)
         load_weights(1)
+        nc.sync.dma_start(out=wgs_t[:, HALF:S], in_=wgs[:, HALF:S])
 
         picked_scales = held.tile([P, S], U8, name="picked_scales")
         nc.vector.tensor_copy(picked_scales[:], scale_window[:].indirect(list1[:]))
@@ -119,69 +120,130 @@ def tile_list_cryogen_board_scores_kernel(
         codes = {}
         planes = {}
 
-        def quantise_weights(b):
-            for a in range(PASSES):
-                rounded = held.tile([P, 2, P, 4], BF16, name=f"rounded{b}{a}", tag=f"rounded{b}{a}", align_bytes=64)
-                for w in range(2):
+        def quantise_weights(b, rounded_tags, codes_tags):
+            for w in range(2):
+                rounded = held.tile([P, PASSES, P, 4], BF16, name=f"rounded{b}{w}", tag=rounded_tags[w], align_bytes=64)
+                for a in range(PASSES):
                     nc.scalar.copy(
-                        rounded[:, w, :, :].rearrange("p (g c) i -> p g i c", c=4),
+                        rounded[:, a, :, :].rearrange("p (g c) i -> p g i c", c=4),
                         raw[b, a, w][:].rearrange("p i (g c) -> p g i c", c=4),
                     )
-                codes[b, a] = held.tile([P, 2 * P], U32, name=f"codes{b}{a}", align_bytes=64)
-                planes[b, a] = held.tile([P, 2 * P], U8, name=f"planes{b}{a}", align_bytes=64)
+                codes[b, w] = held.tile([P, PASSES * P], U32, name=f"codes{b}{w}", tag=codes_tags[w], align_bytes=64)
+                planes[b, w] = held.tile([P, PASSES * P], U8, name=f"planes{b}{w}", align_bytes=64)
                 nc.vector.quantize_mx(
-                    out=codes[b, a][:].bitcast(FP8X4),
-                    scales=planes[b, a][:],
-                    in_=rounded[:].rearrange("p w c i -> p (w c i)"),
+                    out=codes[b, w][:].bitcast(FP8X4),
+                    scales=planes[b, w][:],
+                    in_=rounded[:].rearrange("p a c i -> p (a c i)"),
                 )
 
-        def products(b, hf):
-            banks = [psum.tile([P, HALF], F32, name=f"acc{b}{hf}{n}", tag="acc", bufs=6) for n in range(3)]
-            cols = slice(HALF * hf, HALF * (hf + 1))
-            for a in range(PASSES):
-                stationary = [
-                    (codes[b, a][:, 0:P].bitcast(FP8X4), planes[b, a][:, 0:P]),
-                    (w1_codes[:, a, 2 * P * b : 2 * P * (b + 1)].bitcast(FP4X4), w1_planes[:, a, P * b : P * (b + 1)]),
-                    (codes[b, a][:, P : 2 * P].bitcast(FP8X4), planes[b, a][:, P : 2 * P]),
-                ]
-                for bank, (lhs, lhs_scale) in zip(banks, stationary):
+        def own_tags(stem, b):
+            return [f"{stem}{b}{w}" for w in range(2)]
+
+        def weight_operands(b, a):
+            cols = slice(P * a, P * (a + 1))
+            return {
+                "a": (w1_codes[:, a, 2 * P * b : 2 * P * (b + 1)].bitcast(FP4X4), w1_planes[:, a, P * b : P * (b + 1)]),
+                "b": (codes[b, 0][:, cols].bitcast(FP8X4), planes[b, 0][:, cols]),
+                "e": (codes[b, 1][:, cols].bitcast(FP8X4), planes[b, 1][:, cols]),
+            }
+
+        def product_banks(k):
+            return {n: psum.tile([P, HALF], F32, name=f"bank_{n}{k}", tag=f"{n}{k % 2}") for n in "abe"}
+
+        def gate(k, banks, tanh_tile):
+            abs_a = work.tile([P, HALF], F32, name=f"abs_a{k}", tag="abs_a", bufs=3)
+            nc.scalar.activation(tanh_tile[:], banks["b"][:], ACT.Tanh)
+            nc.scalar.activation(abs_a[:], banks["a"][:], ACT.Abs)
+            return abs_a
+
+        def products_rows(k, tanh_tile):
+            b, hf = divmod(k, 2)
+            banks = product_banks(k)
+            for n in "abe":
+                for a in range(PASSES):
+                    lhs, lhs_scale = weight_operands(b, a)[n]
                     nc.tensor.matmul_mx(
-                        out=bank[:], lhsT=lhs, lhsT_scale=lhs_scale,
-                        rhs=picked[a, hf][:].bitcast(FP8X4), rhs_scale=tab_planes[a][:, cols],
+                        out=banks[n][:], lhsT=lhs, lhsT_scale=lhs_scale,
+                        rhs=picked[a, hf][:].bitcast(FP8X4), rhs_scale=tab_planes[a][:, HALF * hf : HALF * (hf + 1)],
                         start=(a == 0), stop=(a == PASSES - 1),
                     )
-            tanh_b = work.tile([P, HALF], F32, name=f"tanh_b{b}{hf}", tag="tanh_b")
-            nc.scalar.activation(tanh_b[:], banks[0][:], ACT.Tanh)
-            abs_a = work.tile([P, HALF], F32, name=f"abs_a{b}{hf}", tag="abs_a")
-            nc.scalar.activation(abs_a[:], banks[1][:], ACT.Abs)
-            return abs_a, tanh_b, banks[2]
+            abs_a = gate(k, banks, tanh_tile)
+            nc.vector.tensor_tensor(abs_a[:], abs_a[:], tanh_tile[:], ALU.mult)
+            return abs_a, banks["e"]
 
-        quantise_weights(0)
-        for b in range(TILES):
-            parts = [products(b, hf) for hf in range(2)]
-            for abs_a, tanh_b, e_bank in parts:
-                nc.vector.tensor_tensor(abs_a[:], abs_a[:], tanh_b[:], ALU.mult)
-            if b == 0:
-                load_weights(2)
-                load_page(1)
-            if b == 1:
-                load_weights(3)
-                load_page(2)
-                load_page(3)
-            hs = []
-            for hf in range(2):
-                if hf == 1 and b + 1 < TILES:
-                    quantise_weights(b + 1)
-                    h = held.tile([P, HALF], F32, name=f"h{b}{hf}", tag=f"rounded{b + 1}1", align_bytes=64)
-                else:
-                    h = work.tile([P, HALF], F32, name=f"h{b}{hf}", tag="h")
-                nc.vector.tensor_tensor(h[:], parts[hf][0][:], parts[hf][2][:], ALU.add)
-                hs.append(h)
-            for hf in range(2):
-                cols = slice(HALF * hf, HALF * (hf + 1))
-                nc.vector.tensor_tensor(
-                    pages[b][:].indirect(entries(list2, HALF * hf, HALF)), hs[hf][:], wgs_t[:, cols], ALU.mult
-                )
+        def products_turned(k, tanh_tile):
+            b, hf = divmod(k, 2)
+            banks = product_banks(k)
+            for n in "bae":
+                for jb in range(HALF // P):
+                    j0 = HALF * hf + P * jb
+                    for a in range(PASSES):
+                        rhs, rhs_scale = weight_operands(b, a)[n]
+                        nc.tensor.matmul_mx(
+                            out=banks[n][:, P * jb : P * (jb + 1)],
+                            lhsT=picked[a, hf][:, P * jb : P * (jb + 1)].bitcast(FP8X4),
+                            lhsT_scale=tab_planes[a][:, j0 : j0 + P],
+                            rhs=rhs, rhs_scale=rhs_scale, start=(a == 0), stop=(a == PASSES - 1),
+                        )
+            abs_a = gate(k, banks, tanh_tile)
+            e_sb = work.tile([P, HALF], F32, name=f"e_sb{k}", tag="e_sb")
+            nc.scalar.copy(e_sb[:], banks["e"][:])
+            nc.vector.tensor_tensor(abs_a[:], abs_a[:], tanh_tile[:], ALU.mult)
+            return abs_a, e_sb
+
+        def sum_turned_back(k, gated, e_sb):
+            if k + 1 < 2 * TILES:
+                bank = psum.tile([P, HALF], F32, name=f"h_bank{k}", tag=f"a{(k + 1) % 2}")
+            else:
+                bank = psum.tile([P, HALF], F32, name=f"h_bank{k}", tag="turn", bufs=2)
+            for term in (e_sb, gated):
+                for jb in range(HALF // P):
+                    cols = slice(P * jb, P * (jb + 1))
+                    nc.tensor.matmul(
+                        bank[:, cols], lhsT=term[:, cols], rhs=ident[:], is_transpose=True,
+                        start=(term is e_sb and jb == 0), stop=(term is gated and jb == HALF // P - 1),
+                    )
+            h = work.tile([P, HALF], F32, name=f"h{k}", tag="h")
+            nc.scalar.copy(h[:], bank[:])
+            return h
+
+        def scatter(b, first, h):
+            count = h.shape[1]
+            nc.vector.tensor_tensor(
+                pages[b][:].indirect(entries(list2, first, count)), h, wgs_t[:, first : first + count], ALU.mult
+            )
+
+        def shared(name, tag, width):
+            return held.tile([P, width], F32, name=name, tag=tag, align_bytes=64)
+
+        quantise_weights(0, own_tags("rounded", 0), own_tags("codes", 0))
+        gated0, e0 = products_rows(0, shared("tanh_b0", "t0", HALF))
+        gated1, e1 = products_rows(1, shared("tanh_b1", "t1", HALF))
+        load_weights(2)
+        load_page(1)
+        h0 = shared("h0", "h0", HALF)
+        nc.vector.tensor_tensor(h0[:], gated0[:], e0[:], ALU.add)
+        scatter(0, 0, h0[:])
+        quantise_weights(1, ["t0", "t1"], ["h0", "codes11"])
+        load_weights(3)
+        load_page(2)
+        load_page(3)
+        h1a = shared("h1a", "t0", CH)
+        nc.vector.tensor_tensor(h1a[:], gated1[:, 0:CH], e1[:, 0:CH], ALU.add)
+        scatter(0, HALF, h1a[:])
+        terms = products_turned(2, shared("tanh_b2", "t2", HALF))
+        h1b = shared("h1b", "t2", CH)
+        nc.vector.tensor_tensor(h1b[:], gated1[:, CH:HALF], e1[:, CH:HALF], ALU.add)
+        scatter(0, HALF + CH, h1b[:])
+        for k in range(2, 2 * TILES):
+            b, hf = divmod(k, 2)
+            if hf == 0 and b + 1 < TILES:
+                quantise_weights(b + 1, own_tags("rounded", b + 1), own_tags("codes", b + 1))
+            ahead = None
+            if k + 1 < 2 * TILES:
+                ahead = products_turned(k + 1, work.tile([P, HALF], F32, name=f"tanh_b{k + 1}", tag="tanh_b"))
+            scatter(b, HALF * hf, sum_turned_back(k, *terms)[:])
+            terms = ahead
 
         site_t = held.tile([P, TILES, PJ], F32, name="site_t", tag="window0")
         for b in range(TILES):
@@ -228,7 +290,7 @@ def tile_list_cryogen_board_scores_kernel(
                     )
                 nc.scalar.copy(turned[:, jb, :, :, :], bank[:].rearrange("j (p u e) -> j u p e", u=2, e=2))
             words = turned[:].rearrange("j g u p e -> j (g u p e)").bitcast(F32)
-            back = psum.tile([P, CH // P, 2, P], F32, name=f"back{c}", tag="acc", bufs=6)
+            back = psum.tile([P, CH // P, 2, P], F32, name=f"back{c}", tag=f"e{c % 2}")
             for jb in range(CH // P):
                 for u in range(2):
                     w0 = (2 * jb + u) * P
@@ -245,7 +307,7 @@ def tile_list_cryogen_board_scores_kernel(
 
         def finish(c, x_codes, x_plane):
             for pair in range(TILES // 2):
-                y = psum.tile([P, 2, CH], F32, name=f"y{c}{pair}", tag="acc", bufs=6)
+                y = psum.tile([P, 2, CH], F32, name=f"y{c}{pair}", tag=f"{'ab'[c % 2]}{pair}")
                 for i in range(2):
                     n0 = P * (2 * pair + i)
                     nc.tensor.matmul_mx(

@@ -39,58 +39,87 @@ def tile_list_cryogen_board_scores_kernel(
             return lst[:, first // 16 : (first + count) // 16]
 
         list1 = held.tile([P, S // 16], U16, name="list1")
-        nc.sync.dma_start(list1[:], offs)
-        scale_window = held.tile([P, T], U8, name="scale_window")
-        nc.sync.dma_start(
-            out=scale_window[0:32, :].bitcast(I32),
-            in_=tab_scales.rearrange("a q t -> (a q) t").bitcast(I32),
-        )
-        nc.vector.memset(scale_window[32:64, :].bitcast(I32), 0)
-        nc.vector.memset(scale_window[64:128, :].bitcast(I32), 0)
+        list2 = held.tile([P, S // 16], U16, name="list2")
+        list3 = held.tile([P, PJ // 16], U16, name="list3")
+        list4 = held.tile([P, PJ // 16], U16, name="list4")
+        picked_scales = held.tile([P, S], U8, name="picked_scales")
+        w1_codes = held.tile([P, PASSES, 2 * H], U8, name="w1_codes", align_bytes=64)
+        w1_planes = held.tile([P, PASSES, H], U8, name="w1_planes", align_bytes=64)
+        tab_planes = [held.tile([P, S], U8, name=f"tab_plane{a}", align_bytes=64) for a in range(PASSES)]
+        nc.gpsimd.memset(w1_planes[:].rearrange("p a c -> p (a c)").bitcast(I32), 0)
+        for a in range(PASSES):
+            nc.gpsimd.memset(tab_planes[a][:].bitcast(I32), 0)
+
+        def table_words(a):
+            return tab_words[a].rearrange("p t i -> p (t i)").bitcast(I32)
+
+        with tc.tile_pool(name="scale_stage", bufs=1) as scale_stage:
+            scale_window = scale_stage.tile([P, T], U8, name="scale_window")
+            nc.sync.dma_start(list1[:], offs)
+            nc.sync.dma_start(
+                out=scale_window[0:32, :].bitcast(I32),
+                in_=tab_scales.rearrange("a q t -> (a q) t").bitcast(I32),
+            )
+            nc.vector.memset(scale_window[32:64, :].bitcast(I32), 0)
+            nc.vector.memset(scale_window[64:128, :].bitcast(I32), 0)
+            nc.sync.dma_start(out=w1_codes[:].bitcast(I32), in_=w1_words.rearrange("a p n -> p a n").bitcast(I32))
+            nc.sync.dma_start(list2[:], offs2)
+            nc.sync.dma_start(list3[:], offs3)
+            nc.sync.dma_start(list4[:], offs4)
+            window0 = held.tile([P, T], I32, name="window0", tag="window0")
+            nc.sync.dma_start(out=window0[:], in_=table_words(0))
+            for q in range(4):
+                nc.sync.dma_start(
+                    out=w1_planes[32 * q : 32 * q + 4, :, :].bitcast(I32),
+                    in_=w1_scales[:, 4 * q : 4 * q + 4, :].rearrange("a r c -> r a c").bitcast(I32),
+                )
+            nc.vector.tensor_copy(picked_scales[:], scale_window[:].indirect(list1[:]))
 
         warm_in = held.tile([P, 1], F32, name="warm_in")
         warm_out = held.tile([P, 1], F32, name="warm_out")
         nc.vector.memset(warm_in[:], 0.0)
         nc.scalar.activation(warm_out[:], warm_in[:], ACT.Tanh)
 
-        w1_planes = held.tile([P, PASSES, H], U8, name="w1_planes", align_bytes=64)
-        nc.gpsimd.memset(w1_planes[:].rearrange("p a c -> p (a c)").bitcast(I32), 0)
-        tab_planes = [held.tile([P, S], U8, name=f"tab_plane{a}", align_bytes=64) for a in range(PASSES)]
-        for a in range(PASSES):
-            nc.gpsimd.memset(tab_planes[a][:].bitcast(I32), 0)
-        w4_plane = held.tile([P, H], U8, name="w4_plane", align_bytes=64)
-        nc.gpsimd.memset(w4_plane[:].bitcast(I32), 0)
+        late = ctx.enter_context(tc.tile_pool(name="late", bufs=1))
+        window1 = late.tile([P, T], I32, name="window1")
+        word_windows = [window0, window1]
 
-        word_windows = [held.tile([P, T], I32, name=f"word_window{a}", tag=f"window{a}") for a in range(PASSES)]
+        def load_window1(quarter):
+            cols = slice(T // 4 * quarter, T // 4 * (quarter + 1))
+            nc.sync.dma_start(out=window1[:, cols], in_=table_words(1)[:, cols])
 
-        def load_words(a):
-            nc.sync.dma_start(out=word_windows[a][:], in_=tab_words[a].rearrange("p t i -> p (t i)").bitcast(I32))
+        def place_scale_rows(a):
+            for q in range(4):
+                nc.sync.dma_start(
+                    out=tab_planes[a][32 * q : 32 * q + 4, :].bitcast(I32),
+                    in_=picked_scales[16 * a + 4 * q : 16 * a + 4 * q + 4, :].bitcast(I32),
+                )
 
         raw = {}
 
-        def load_weights(b):
-            for w, weight in enumerate((w2, w3)):
-                for a in range(PASSES):
-                    t = work.tile([P, 4, P], F32, name=f"raw{b}{a}{w}", tag="raw", bufs=8)
-                    rows = weight[512 * a : 512 * (a + 1), P * b : P * (b + 1)]
-                    nc.sync.dma_start(out=t[:], in_=rows.rearrange("(p i) c -> p i c", i=4))
-                    raw[b, a, w] = t
+        def load_weight_rows(b, w, a):
+            t = late.tile([P, 4, P], F32, name=f"raw{b}{a}{w}", tag=f"raw{b}{a}{w}", align_bytes=64)
+            rows = (w2, w3)[w][512 * a : 512 * (a + 1), P * b : P * (b + 1)]
+            nc.sync.dma_start(out=t[:], in_=rows.rearrange("(p i) c -> p i c", i=4))
+            raw[b, a, w] = t
 
-        load_words(0)
-        load_words(1)
-        w1_codes = held.tile([P, PASSES, 2 * H], U8, name="w1_codes", align_bytes=64)
-        nc.sync.dma_start(out=w1_codes[:].bitcast(I32), in_=w1_words.rearrange("a p n -> p a n").bitcast(I32))
-        load_weights(0)
-        for q in range(4):
-            nc.gpsimd.dma_start(
-                out=w1_planes[32 * q : 32 * q + 4, :, :].bitcast(I32),
-                in_=w1_scales[:, 4 * q : 4 * q + 4, :].rearrange("a r c -> r a c").bitcast(I32),
-            )
-        list2 = held.tile([P, S // 16], U16, name="list2")
-        nc.sync.dma_start(list2[:], offs2)
-        wgs_t = held.tile([P, S], F32, name="wgs_t", tag="wgs_then_picks")
+        def load_weights(b):
+            for w in range(2):
+                for a in range(PASSES):
+                    load_weight_rows(b, w, a)
+
+        for quarter in range(3):
+            load_window1(quarter)
+        place_scale_rows(0)
+        load_window1(3)
+        load_weight_rows(0, 0, 0)
+        place_scale_rows(1)
+        load_weight_rows(0, 0, 1)
+        load_weight_rows(0, 1, 0)
+        load_weight_rows(0, 1, 1)
+        wgs_t = late.tile([P, S], F32, name="wgs_t", tag="wgs_then_picks")
         nc.sync.dma_start(out=wgs_t[:, 0:HALF], in_=wgs[:, 0:HALF])
-        pages = [held.tile([P, T2], F32, name=f"page{b}") for b in range(TILES)]
+        pages = [late.tile([P, T2], F32, name=f"page{b}") for b in range(TILES)]
 
         def load_page(b):
             nc.sync.dma_start(out=pages[b][:], in_=page0[P * b : P * (b + 1), :])
@@ -99,59 +128,61 @@ def tile_list_cryogen_board_scores_kernel(
         load_weights(1)
         nc.sync.dma_start(out=wgs_t[:, HALF:S], in_=wgs[:, HALF:S])
 
-        picked_scales = held.tile([P, S], U8, name="picked_scales")
-        nc.vector.tensor_copy(picked_scales[:], scale_window[:].indirect(list1[:]))
-        for a in range(PASSES):
-            for q in range(4):
-                nc.gpsimd.dma_start(
-                    out=tab_planes[a][32 * q : 32 * q + 4, :].bitcast(I32),
-                    in_=picked_scales[16 * a + 4 * q : 16 * a + 4 * q + 4, :].bitcast(I32),
-                )
         picked = {}
-        for a in range(PASSES):
-            for hf in range(2):
-                t = held.tile([P, HALF], U32, name=f"picked{a}{hf}", align_bytes=64)
-                nc.vector.tensor_copy(t[:], word_windows[a][:].bitcast(U32).indirect(entries(list1, HALF * hf, HALF)))
-                picked[a, hf] = t
+
+        def gather_words(a, hf, tag):
+            t = held.tile([P, HALF], U32, name=f"picked{a}{hf}", tag=tag, align_bytes=64)
+            nc.vector.tensor_copy(t[:], word_windows[a][:].bitcast(U32).indirect(entries(list1, HALF * hf, HALF)))
+            picked[a, hf] = t
+
+        for a, hf in ((0, 0), (0, 1), (1, 0)):
+            gather_words(a, hf, f"picked{a}{hf}")
 
         ident = held.tile([P, P], F32, name="ident")
         make_identity(nc, ident[:])
 
-        codes = {}
-        planes = {}
+        quantised_w = {}
+
+        def quantise_passes(b, w, passes, rounded_tag, codes_tag):
+            n = len(passes)
+            stem = f"{b}{w}{passes[0]}"
+            rounded = held.tile([P, n, P, 4], BF16, name=f"rounded{stem}", tag=rounded_tag, align_bytes=64)
+            for i, a in enumerate(passes):
+                nc.scalar.copy(
+                    rounded[:, i, :, :].rearrange("p (g c) i -> p g i c", c=4),
+                    raw[b, a, w][:].rearrange("p i (g c) -> p g i c", c=4),
+                )
+            words = late.tile([P, n * P], U32, name=f"codes{stem}", tag=codes_tag, align_bytes=64)
+            plane = held.tile([P, n * P], U8, name=f"planes{stem}", align_bytes=64)
+            nc.vector.quantize_mx(
+                out=words[:].bitcast(FP8X4), scales=plane[:], in_=rounded[:].rearrange("p a c i -> p (a c i)")
+            )
+            for i, a in enumerate(passes):
+                cols = slice(P * i, P * (i + 1))
+                quantised_w[b, w, a] = (words[:, cols].bitcast(FP8X4), plane[:, cols])
 
         def quantise_weights(b, rounded_tags, codes_tags):
             for w in range(2):
-                rounded = held.tile([P, PASSES, P, 4], BF16, name=f"rounded{b}{w}", tag=rounded_tags[w], align_bytes=64)
-                for a in range(PASSES):
-                    nc.scalar.copy(
-                        rounded[:, a, :, :].rearrange("p (g c) i -> p g i c", c=4),
-                        raw[b, a, w][:].rearrange("p i (g c) -> p g i c", c=4),
-                    )
-                codes[b, w] = held.tile([P, PASSES * P], U32, name=f"codes{b}{w}", tag=codes_tags[w], align_bytes=64)
-                planes[b, w] = held.tile([P, PASSES * P], U8, name=f"planes{b}{w}", align_bytes=64)
-                nc.vector.quantize_mx(
-                    out=codes[b, w][:].bitcast(FP8X4),
-                    scales=planes[b, w][:],
-                    in_=rounded[:].rearrange("p a c i -> p (a c i)"),
-                )
+                quantise_passes(b, w, list(range(PASSES)), rounded_tags[w], codes_tags[w])
 
         def own_tags(stem, b):
             return [f"{stem}{b}{w}" for w in range(2)]
 
         def weight_operands(b, a):
-            cols = slice(P * a, P * (a + 1))
             return {
                 "a": (w1_codes[:, a, 2 * P * b : 2 * P * (b + 1)].bitcast(FP4X4), w1_planes[:, a, P * b : P * (b + 1)]),
-                "b": (codes[b, 0][:, cols].bitcast(FP8X4), planes[b, 0][:, cols]),
-                "e": (codes[b, 1][:, cols].bitcast(FP8X4), planes[b, 1][:, cols]),
+                "b": quantised_w[b, 0, a],
+                "e": quantised_w[b, 1, a],
             }
 
         def product_banks(k):
             return {n: psum.tile([P, HALF], F32, name=f"bank_{n}{k}", tag=f"{n}{k % 2}") for n in "abe"}
 
         def gate(k, banks, tanh_tile):
-            abs_a = work.tile([P, HALF], F32, name=f"abs_a{k}", tag="abs_a", bufs=3)
+            if k < 2:
+                abs_a = late.tile([P, HALF], F32, name=f"abs_a{k}", tag=("raw011", "abs_a1")[k], align_bytes=64)
+            else:
+                abs_a = work.tile([P, HALF], F32, name=f"abs_a{k}", tag="abs_a", bufs=3)
             nc.scalar.activation(tanh_tile[:], banks["b"][:], ACT.Tanh)
             nc.scalar.activation(abs_a[:], banks["a"][:], ACT.Abs)
             return abs_a
@@ -167,9 +198,7 @@ def tile_list_cryogen_board_scores_kernel(
                         rhs=picked[a, hf][:].bitcast(FP8X4), rhs_scale=tab_planes[a][:, HALF * hf : HALF * (hf + 1)],
                         start=(a == 0), stop=(a == PASSES - 1),
                     )
-            abs_a = gate(k, banks, tanh_tile)
-            nc.vector.tensor_tensor(abs_a[:], abs_a[:], tanh_tile[:], ALU.mult)
-            return abs_a, banks["e"]
+            return gate(k, banks, tanh_tile), banks["e"]
 
         def products_turned(k, tanh_tile):
             b, hf = divmod(k, 2)
@@ -216,15 +245,24 @@ def tile_list_cryogen_board_scores_kernel(
         def shared(name, tag, width):
             return held.tile([P, width], F32, name=name, tag=tag, align_bytes=64)
 
-        quantise_weights(0, own_tags("rounded", 0), own_tags("codes", 0))
-        gated0, e0 = products_rows(0, shared("tanh_b0", "t0", HALF))
-        gated1, e1 = products_rows(1, shared("tanh_b1", "t1", HALF))
+        for a in range(PASSES):
+            quantise_passes(0, 0, [a], f"rounded00{a}", f"codes00{a}")
+        for a in range(PASSES):
+            quantise_passes(0, 1, [a], f"rounded01{a}", f"codes01{a}")
+        gather_words(1, 1, "rounded011")
+        tanh0 = shared("tanh_b0", "t0", HALF)
+        gated0, e0 = products_rows(0, tanh0)
+        nc.vector.tensor_tensor(gated0[:], gated0[:], tanh0[:], ALU.mult)
+        h0 = late.tile([P, HALF], F32, name="h0", tag="h0", align_bytes=64)
+        nc.vector.tensor_tensor(h0[:], gated0[:], e0[:], ALU.add)
+        tanh1 = shared("tanh_b1", "t1", HALF)
+        abs1, e1 = products_rows(1, tanh1)
         load_weights(2)
         load_page(1)
-        h0 = shared("h0", "h0", HALF)
-        nc.vector.tensor_tensor(h0[:], gated0[:], e0[:], ALU.add)
         scatter(0, 0, h0[:])
-        quantise_weights(1, ["t0", "t1"], ["h0", "codes11"])
+        gated1 = late.tile([P, HALF], F32, name="gated1", tag="h0", align_bytes=64)
+        nc.vector.tensor_tensor(gated1[:], abs1[:], tanh1[:], ALU.mult)
+        quantise_weights(1, ["t0", "t1"], ["abs_a1", "codes11"])
         load_weights(3)
         load_page(2)
         load_page(3)
@@ -248,24 +286,22 @@ def tile_list_cryogen_board_scores_kernel(
         site_t = held.tile([P, TILES, PJ], F32, name="site_t", tag="window0")
         for b in range(TILES):
             nc.sync.dma_start(out=site_t[:, b, :], in_=site[P * b : P * (b + 1), :])
-        list3 = held.tile([P, PJ // 16], U16, name="list3")
-        nc.sync.dma_start(list3[:], offs3)
-        list4 = held.tile([P, PJ // 16], U16, name="list4")
-        nc.sync.dma_start(list4[:], offs4)
-        w4_codes = held.tile([P, H], I32, name="w4_codes", align_bytes=64)
+        w4_plane = late.tile([P, H], U8, name="w4_plane", align_bytes=64)
+        nc.gpsimd.memset(w4_plane[:].bitcast(I32), 0)
+        w4_codes = late.tile([P, H], I32, name="w4_codes", align_bytes=64)
         nc.sync.dma_start(out=w4_codes[:], in_=w4_words[0].rearrange("p c i -> p (c i)").bitcast(I32))
         for q in range(4):
             nc.sync.dma_start(
                 out=w4_plane[32 * q : 32 * q + 4, :].bitcast(I32),
                 in_=w4_scales[0, 4 * q : 4 * q + 4, :].bitcast(I32),
             )
-        gx_t = held.tile([P, TILES], F32, name="gx_t")
-        gy_t = held.tile([P, TILES], F32, name="gy_t")
+        gx_t = late.tile([P, TILES], F32, name="gx_t")
+        gy_t = late.tile([P, TILES], F32, name="gy_t")
         with nc.allow_non_contiguous_dma(reason="one gain a partition"):
             nc.sync.dma_start(out=gx_t[:], in_=gx.rearrange("(b p) -> p b", p=P))
             nc.sync.dma_start(out=gy_t[:], in_=gy.rearrange("(b p) -> p b", p=P))
 
-        first_picks = held.tile([P, (CHUNKS - 1) * TILES, CH], F32, name="first_picks", tag="wgs_then_picks")
+        first_picks = late.tile([P, (CHUNKS - 1) * TILES, CH], F32, name="first_picks", tag="wgs_then_picks")
 
         def gather_x(c, picks):
             for b in range(TILES):

from contextlib import ExitStack

import concourse.mybir as mybir
from concourse.masks import make_identity

K, H, T, S, T2, PJ = 1024, 512, 4096, 1024, 2048, 1024
FLOPS = 2 * (3 * K * H * S + H * H * PJ)

F32 = mybir.dt.float32
BF16 = mybir.dt.bfloat16
I32 = mybir.dt.int32
U32 = mybir.dt.uint32
U16 = mybir.dt.uint16
U8 = mybir.dt.uint8
FP8X4 = mybir.dt.float8_e4m3fn_x4
FP4X4 = mybir.dt.float4_e2m1fn_x4
ACT = mybir.ActivationFunctionType
ALU = mybir.AluOpType

P = 128
PASSES = K // 512
TILES = H // P
HALF = 512
CH = 256
CHUNKS = PJ // CH


def tile_list_cryogen_board_scores_kernel(
    tc, tab_words, tab_scales, offs, w1_words, w1_scales, w2, w3, wgs, page0,
    offs2, offs3, offs4, gx, site, w4_words, w4_scales, gy, out,
):
    nc = tc.nc
    with ExitStack() as ctx:
        held = ctx.enter_context(tc.tile_pool(name="held", bufs=1))
        work = ctx.enter_context(tc.tile_pool(name="work", bufs=2))
        psum = ctx.enter_context(tc.psum_pool(name="psum", bufs=1))

        def entries(lst, first, count):
            return lst[:, first // 16 : (first + count) // 16]

        list1 = held.tile([P, S // 16], U16, name="list1")
        list2 = held.tile([P, S // 16], U16, name="list2")
        list3 = held.tile([P, PJ // 16], U16, name="list3")
        list4 = held.tile([P, PJ // 16], U16, name="list4")
        picked_scales = held.tile([P, S], U8, name="picked_scales")
        w1_codes = held.tile([P, PASSES, 2 * H], U8, name="w1_codes", align_bytes=64)
        w1_planes = held.tile([P, PASSES, H], U8, name="w1_planes", align_bytes=64)
        tab_planes = [held.tile([P, S], U8, name=f"tab_plane{a}", align_bytes=64) for a in range(PASSES)]
        nc.gpsimd.memset(w1_planes[:].rearrange("p a c -> p (a c)").bitcast(I32), 0)
        for a in range(PASSES):
            nc.gpsimd.memset(tab_planes[a][:].bitcast(I32), 0)

        def table_words(a):
            return tab_words[a].rearrange("p t i -> p (t i)").bitcast(I32)

        with tc.tile_pool(name="scale_stage", bufs=1) as scale_stage:
            scale_window = scale_stage.tile([P, T], U8, name="scale_window")
            nc.sync.dma_start(list1[:], offs)
            nc.sync.dma_start(
                out=scale_window[0:32, :].bitcast(I32),
                in_=tab_scales.rearrange("a q t -> (a q) t").bitcast(I32),
            )
            nc.vector.memset(scale_window[32:64, :].bitcast(I32), 0)
            nc.vector.memset(scale_window[64:128, :].bitcast(I32), 0)
            nc.sync.dma_start(out=w1_codes[:].bitcast(I32), in_=w1_words.rearrange("a p n -> p a n").bitcast(I32))
            nc.sync.dma_start(list2[:], offs2)
            nc.sync.dma_start(list3[:], offs3)
            nc.sync.dma_start(list4[:], offs4)
            window0 = held.tile([P, T], I32, name="window0", tag="window0")
            nc.sync.dma_start(out=window0[:], in_=table_words(0))
            for q in range(4):
                nc.sync.dma_start(
                    out=w1_planes[32 * q : 32 * q + 4, :, :].bitcast(I32),
                    in_=w1_scales[:, 4 * q : 4 * q + 4, :].rearrange("a r c -> r a c").bitcast(I32),
                )
            nc.vector.tensor_copy(picked_scales[:], scale_window[:].indirect(list1[:]))

        warm_in = held.tile([P, 1], F32, name="warm_in")
        warm_out = held.tile([P, 1], F32, name="warm_out")
        nc.vector.memset(warm_in[:], 0.0)
        nc.scalar.activation(warm_out[:], warm_in[:], ACT.Tanh)

        late = ctx.enter_context(tc.tile_pool(name="late", bufs=1))
        window1 = late.tile([P, T], I32, name="window1")
        word_windows = [window0, window1]

        def load_window1(quarter):
            cols = slice(T // 4 * quarter, T // 4 * (quarter + 1))
            nc.sync.dma_start(out=window1[:, cols], in_=table_words(1)[:, cols])

        def place_scale_rows(a):
            for q in range(4):
                nc.sync.dma_start(
                    out=tab_planes[a][32 * q : 32 * q + 4, :].bitcast(I32),
                    in_=picked_scales[16 * a + 4 * q : 16 * a + 4 * q + 4, :].bitcast(I32),
                )

        raw = {}

        def load_weight_rows(b, w, a):
            t = late.tile([P, 4, P], F32, name=f"raw{b}{a}{w}", tag=f"raw{b}{a}{w}", align_bytes=64)
            rows = (w2, w3)[w][512 * a : 512 * (a + 1), P * b : P * (b + 1)]
            nc.sync.dma_start(out=t[:], in_=rows.rearrange("(p i) c -> p i c", i=4))
            raw[b, a, w] = t

        def load_weights(b):
            for w in range(2):
                for a in range(PASSES):
                    load_weight_rows(b, w, a)

        for quarter in range(3):
            load_window1(quarter)
        place_scale_rows(0)
        load_window1(3)
        load_weight_rows(0, 0, 0)
        place_scale_rows(1)
        load_weight_rows(0, 0, 1)
        load_weight_rows(0, 1, 0)
        load_weight_rows(0, 1, 1)
        wgs_t = late.tile([P, S], F32, name="wgs_t", tag="wgs_then_picks")
        nc.sync.dma_start(out=wgs_t[:, 0:HALF], in_=wgs[:, 0:HALF])
        pages = [late.tile([P, T2], F32, name=f"page{b}") for b in range(TILES)]

        def load_page(b):
            nc.sync.dma_start(out=pages[b][:], in_=page0[P * b : P * (b + 1), :])

        load_page(0)
        load_weights(1)
        nc.sync.dma_start(out=wgs_t[:, HALF:S], in_=wgs[:, HALF:S])

        picked = {}

        def gather_words(a, hf, tag):
            t = held.tile([P, HALF], U32, name=f"picked{a}{hf}", tag=tag, align_bytes=64)
            nc.vector.tensor_copy(t[:], word_windows[a][:].bitcast(U32).indirect(entries(list1, HALF * hf, HALF)))
            picked[a, hf] = t

        for a, hf in ((0, 0), (0, 1), (1, 0)):
            gather_words(a, hf, f"picked{a}{hf}")

        ident = held.tile([P, P], F32, name="ident")
        make_identity(nc, ident[:])

        quantised_w = {}

        def quantise_passes(b, w, passes, rounded_tag, codes_tag):
            n = len(passes)
            stem = f"{b}{w}{passes[0]}"
            rounded = held.tile([P, n, P, 4], BF16, name=f"rounded{stem}", tag=rounded_tag, align_bytes=64)
            for i, a in enumerate(passes):
                nc.scalar.copy(
                    rounded[:, i, :, :].rearrange("p (g c) i -> p g i c", c=4),
                    raw[b, a, w][:].rearrange("p i (g c) -> p g i c", c=4),
                )
            words = late.tile([P, n * P], U32, name=f"codes{stem}", tag=codes_tag, align_bytes=64)
            plane = held.tile([P, n * P], U8, name=f"planes{stem}", align_bytes=64)
            nc.vector.quantize_mx(
                out=words[:].bitcast(FP8X4), scales=plane[:], in_=rounded[:].rearrange("p a c i -> p (a c i)")
            )
            for i, a in enumerate(passes):
                cols = slice(P * i, P * (i + 1))
                quantised_w[b, w, a] = (words[:, cols].bitcast(FP8X4), plane[:, cols])

        def quantise_weights(b, rounded_tags, codes_tags):
            for w in range(2):
                quantise_passes(b, w, list(range(PASSES)), rounded_tags[w], codes_tags[w])

        def own_tags(stem, b):
            return [f"{stem}{b}{w}" for w in range(2)]

        def weight_operands(b, a):
            return {
                "a": (w1_codes[:, a, 2 * P * b : 2 * P * (b + 1)].bitcast(FP4X4), w1_planes[:, a, P * b : P * (b + 1)]),
                "b": quantised_w[b, 0, a],
                "e": quantised_w[b, 1, a],
            }

        def product_banks(k):
            return {n: psum.tile([P, HALF], F32, name=f"bank_{n}{k}", tag=f"{n}{k % 2}") for n in "abe"}

        def gate(k, banks, tanh_tile):
            if k < 2:
                abs_a = late.tile([P, HALF], F32, name=f"abs_a{k}", tag=("raw011", "abs_a1")[k], align_bytes=64)
            else:
                abs_a = work.tile([P, HALF], F32, name=f"abs_a{k}", tag="abs_a", bufs=3)
            nc.scalar.activation(tanh_tile[:], banks["b"][:], ACT.Tanh)
            nc.scalar.activation(abs_a[:], banks["a"][:], ACT.Abs)
            return abs_a

        def products_rows(k, tanh_tile):
            b, hf = divmod(k, 2)
            banks = product_banks(k)
            for n in "abe":
                for a in range(PASSES):
                    lhs, lhs_scale = weight_operands(b, a)[n]
                    nc.tensor.matmul_mx(
                        out=banks[n][:], lhsT=lhs, lhsT_scale=lhs_scale,
                        rhs=picked[a, hf][:].bitcast(FP8X4), rhs_scale=tab_planes[a][:, HALF * hf : HALF * (hf + 1)],
                        start=(a == 0), stop=(a == PASSES - 1),
                    )
            return gate(k, banks, tanh_tile), banks["e"]

        def products_turned(k, tanh_tile):
            b, hf = divmod(k, 2)
            banks = product_banks(k)
            for n in "bae":
                for jb in range(HALF // P):
                    j0 = HALF * hf + P * jb
                    for a in range(PASSES):
                        rhs, rhs_scale = weight_operands(b, a)[n]
                        nc.tensor.matmul_mx(
                            out=banks[n][:, P * jb : P * (jb + 1)],
                            lhsT=picked[a, hf][:, P * jb : P * (jb + 1)].bitcast(FP8X4),
                            lhsT_scale=tab_planes[a][:, j0 : j0 + P],
                            rhs=rhs, rhs_scale=rhs_scale, start=(a == 0), stop=(a == PASSES - 1),
                        )
            abs_a = gate(k, banks, tanh_tile)
            e_sb = work.tile([P, HALF], F32, name=f"e_sb{k}", tag="e_sb")
            nc.scalar.copy(e_sb[:], banks["e"][:])
            nc.vector.tensor_tensor(abs_a[:], abs_a[:], tanh_tile[:], ALU.mult)
            return abs_a, e_sb

        def sum_turned_back(k, gated, e_sb):
            if k + 1 < 2 * TILES:
                bank = psum.tile([P, HALF], F32, name=f"h_bank{k}", tag=f"a{(k + 1) % 2}")
            else:
                bank = psum.tile([P, HALF], F32, name=f"h_bank{k}", tag="turn", bufs=2)
            for term in (e_sb, gated):
                for jb in range(HALF // P):
                    cols = slice(P * jb, P * (jb + 1))
                    nc.tensor.matmul(
                        bank[:, cols], lhsT=term[:, cols], rhs=ident[:], is_transpose=True,
                        start=(term is e_sb and jb == 0), stop=(term is gated and jb == HALF // P - 1),
                    )
            h = work.tile([P, HALF], F32, name=f"h{k}", tag="h")
            nc.scalar.copy(h[:], bank[:])
            return h

        def scatter(b, first, h):
            count = h.shape[1]
            nc.vector.tensor_tensor(
                pages[b][:].indirect(entries(list2, first, count)), h, wgs_t[:, first : first + count], ALU.mult
            )

        def shared(name, tag, width):
            return held.tile([P, width], F32, name=name, tag=tag, align_bytes=64)

        for a in range(PASSES):
            quantise_passes(0, 0, [a], f"rounded00{a}", f"codes00{a}")
        for a in range(PASSES):
            quantise_passes(0, 1, [a], f"rounded01{a}", f"codes01{a}")
        gather_words(1, 1, "rounded011")
        tanh0 = shared("tanh_b0", "t0", HALF)
        gated0, e0 = products_rows(0, tanh0)
        nc.vector.tensor_tensor(gated0[:], gated0[:], tanh0[:], ALU.mult)
        h0 = late.tile([P, HALF], F32, name="h0", tag="h0", align_bytes=64)
        nc.vector.tensor_tensor(h0[:], gated0[:], e0[:], ALU.add)
        tanh1 = shared("tanh_b1", "t1", HALF)
        abs1, e1 = products_rows(1, tanh1)
        load_weights(2)
        load_page(1)
        scatter(0, 0, h0[:])
        gated1 = late.tile([P, HALF], F32, name="gated1", tag="h0", align_bytes=64)
        nc.vector.tensor_tensor(gated1[:], abs1[:], tanh1[:], ALU.mult)
        quantise_weights(1, ["t0", "t1"], ["abs_a1", "codes11"])
        load_weights(3)
        load_page(2)
        load_page(3)
        h1a = shared("h1a", "t0", CH)
        nc.vector.tensor_tensor(h1a[:], gated1[:, 0:CH], e1[:, 0:CH], ALU.add)
        scatter(0, HALF, h1a[:])
        terms = products_turned(2, shared("tanh_b2", "t2", HALF))
        h1b = shared("h1b", "t2", CH)
        nc.vector.tensor_tensor(h1b[:], gated1[:, CH:HALF], e1[:, CH:HALF], ALU.add)
        scatter(0, HALF + CH, h1b[:])
        for k in range(2, 2 * TILES):
            b, hf = divmod(k, 2)
            if hf == 0 and b + 1 < TILES:
                quantise_weights(b + 1, own_tags("rounded", b + 1), own_tags("codes", b + 1))
            ahead = None
            if k + 1 < 2 * TILES:
                ahead = products_turned(k + 1, work.tile([P, HALF], F32, name=f"tanh_b{k + 1}", tag="tanh_b"))
            scatter(b, HALF * hf, sum_turned_back(k, *terms)[:])
            terms = ahead

        site_t = held.tile([P, TILES, PJ], F32, name="site_t", tag="window0")
        for b in range(TILES):
            nc.sync.dma_start(out=site_t[:, b, :], in_=site[P * b : P * (b + 1), :])
        w4_plane = late.tile([P, H], U8, name="w4_plane", align_bytes=64)
        nc.gpsimd.memset(w4_plane[:].bitcast(I32), 0)
        w4_codes = late.tile([P, H], I32, name="w4_codes", align_bytes=64)
        nc.sync.dma_start(out=w4_codes[:], in_=w4_words[0].rearrange("p c i -> p (c i)").bitcast(I32))
        for q in range(4):
            nc.sync.dma_start(
                out=w4_plane[32 * q : 32 * q + 4, :].bitcast(I32),
                in_=w4_scales[0, 4 * q : 4 * q + 4, :].bitcast(I32),
            )
        gx_t = late.tile([P, TILES], F32, name="gx_t")
        gy_t = late.tile([P, TILES], F32, name="gy_t")
        with nc.allow_non_contiguous_dma(reason="one gain a partition"):
            nc.sync.dma_start(out=gx_t[:], in_=gx.rearrange("(b p) -> p b", p=P))
            nc.sync.dma_start(out=gy_t[:], in_=gy.rearrange("(b p) -> p b", p=P))

        first_picks = late.tile([P, (CHUNKS - 1) * TILES, CH], F32, name="first_picks", tag="wgs_then_picks")

        def gather_x(c, picks):
            for b in range(TILES):
                nc.vector.tensor_copy(picks[b], pages[b][:].indirect(entries(list3, CH * c, CH)))

        def make_x(c, picks):
            for b in range(TILES):
                nc.scalar.activation(picks[b], picks[b], ACT.Copy, scale=gx_t[:, b : b + 1])
            turned = work.tile([P, CH // P, 2, P, 2], BF16, name=f"turned{c}", tag="turned")
            for jb in range(CH // P):
                bank = psum.tile([P, H], F32, name=f"turn{c}{jb}", tag="turn", bufs=2)
                j0 = CH * c + P * jb
                for b in range(TILES):
                    nc.tensor.matmul(
                        bank[:, P * b : P * (b + 1)], lhsT=site_t[:, b, j0 : j0 + P], rhs=ident[:],
                        is_transpose=True, start=(b == 0), stop=False,
                    )
                for b in range(TILES):
                    nc.tensor.matmul(
                        bank[:, P * b : P * (b + 1)], lhsT=picks[b][:, P * jb : P * (jb + 1)], rhs=ident[:],
                        is_transpose=True, start=False, stop=(b == TILES - 1),
                    )
                nc.scalar.copy(turned[:, jb, :, :, :], bank[:].rearrange("j (p u e) -> j u p e", u=2, e=2))
            words = turned[:].rearrange("j g u p e -> j (g u p e)").bitcast(F32)
            back = psum.tile([P, CH // P, 2, P], F32, name=f"back{c}", tag=f"e{c % 2}")
            for jb in range(CH // P):
                for u in range(2):
                    w0 = (2 * jb + u) * P
                    nc.tensor.transpose(back[:, jb, u, :], words[:, w0 : w0 + P], ident[:])
            x_in = held.tile([P, 4 * CH], BF16, name=f"x_in{c}", tag=f"x_in{c}", align_bytes=64)
            nc.scalar.copy(
                x_in[:].bitcast(F32).rearrange("p (g j u) -> p g j u", j=P, u=2),
                back[:].rearrange("p g u j -> p g j u"),
            )
            x_codes = held.tile([P, CH], U32, name=f"x_codes{c}", align_bytes=64)
            x_plane = held.tile([P, CH], U8, name=f"x_plane{c}", align_bytes=64)
            nc.vector.quantize_mx(out=x_codes[:].bitcast(FP8X4), scales=x_plane[:], in_=x_in[:])
            return x_codes, x_plane

        def finish(c, x_codes, x_plane):
            for pair in range(TILES // 2):
                y = psum.tile([P, 2, CH], F32, name=f"y{c}{pair}", tag=f"{'ab'[c % 2]}{pair}")
                for i in range(2):
                    n0 = P * (2 * pair + i)
                    nc.tensor.matmul_mx(
                        out=y[:, i, :], lhsT=w4_codes[:, n0 : n0 + P].bitcast(FP8X4), lhsT_scale=w4_plane[:, n0 : n0 + P],
                        rhs=x_codes[:].bitcast(FP8X4), rhs_scale=x_plane[:], start=True, stop=True,
                    )
                tanh_y = work.tile([P, 2, CH], F32, name=f"tanh_y{c}{pair}", tag="tanh_y", bufs=4)
                nc.scalar.activation(tanh_y[:], y[:], ACT.Tanh)
                peer = work.tile([P, 2, CH], F32, name=f"peer{c}{pair}", tag="peer")
                for i in range(2):
                    nc.vector.tensor_tensor(
                        peer[:, i, :], pages[2 * pair + i][:].indirect(entries(list4, CH * c, CH)), tanh_y[:, i, :], ALU.mult
                    )
                for i in range(2):
                    n = 2 * pair + i
                    res = work.tile([P, CH], F32, name=f"res{c}{n}", tag="res", bufs=8)
                    nc.vector.scalar_tensor_tensor(
                        res[:], peer[:, i, :], gy_t[:, n : n + 1], y[:, i, :], ALU.mult, ALU.add
                    )
                    nc.sync.dma_start(out=out[P * n : P * (n + 1), CH * c : CH * (c + 1)], in_=res[:])

        picks = {c: [first_picks[:, TILES * c + b, :] for b in range(TILES)] for c in range(CHUNKS - 1)}
        for c in range(CHUNKS - 1):
            gather_x(c, picks[c])
        quantised = {0: make_x(0, picks[0])}
        last_picks = held.tile([P, TILES, CH], F32, name="last_picks", tag="x_in0", align_bytes=64)
        picks[CHUNKS - 1] = [last_picks[:, b, :] for b in range(TILES)]
        gather_x(CHUNKS - 1, picks[CHUNKS - 1])
        for c in range(CHUNKS):
            if c + 1 < CHUNKS:
                quantised[c + 1] = make_x(c + 1, picks[c + 1])
            finish(c, *quantised[c])
